import numpy as np
import ml_dtypes


def mxq(x, axis, fmt="e4m3"):
    dtype, down = {"e4m3": (ml_dtypes.float8_e4m3fn, 7), "e5m2": (ml_dtypes.float8_e5m2, 14)}[fmt]
    v = np.moveaxis(np.asarray(x, np.float32).astype(ml_dtypes.bfloat16).astype(np.float64), axis, -1)
    blocks = v.reshape(v.shape[:-1] + (-1, 32))
    amax = np.abs(blocks).max(-1, keepdims=True)
    byte = np.maximum(np.where(amax > 0, np.frexp(amax)[1] - 1 + 127, 0) - down, 1)
    scale = np.exp2(byte - 127.0)
    codes = (blocks / scale).astype(np.float32).astype(dtype).astype(np.float64)
    return np.moveaxis((codes * scale).reshape(v.shape), -1, axis)


WIDE = False


def mx_kscale(k):
    if not WIDE:
        return np.ones(k)
    levels = np.array([10, -10, 5, -5, 0])
    if k % 512:
        return np.exp2(np.random.permutation(np.resize(levels, k // 32))).repeat(32)
    a = np.empty((k // 512, 16))
    for p in range(k // 512):
        a[p, :8] = np.random.permutation(np.resize(levels, 8))
        for g in range(8):
            far = levels[np.abs(levels - a[p, g]) >= 10]
            a[p, g + 8] = far[np.random.randint(len(far))]
    return np.exp2(a.ravel()).repeat(32)


def f64(x):
    return np.asarray(x).astype(np.float64)


def striped(idx):
    return np.tile(np.asarray(idx).reshape(-1, 16).T, (8, 1)).astype(np.uint16)


def unstriped(offs):
    return offs[:16].T.reshape(-1).astype(np.int64)


E2M1 = np.array([0.0, 0.5, 1.0, 1.5, 2.0, 3.0, 4.0, 6.0, -0.0, -0.5, -1.0, -1.5, -2.0, -3.0, -4.0, -6.0])


def pack_weight(w, fmt):
    k, n = w.shape
    w = f64(np.asarray(w, np.float32).astype(ml_dtypes.bfloat16)).reshape(k // 32, 32, n)
    amax = np.abs(w).max(1)
    if fmt == "e4m3":
        byte = np.frexp(amax)[1] - 1 + 127 - 7
    else:
        mant, ex = np.frexp(amax / 6.0)
        byte = np.where(mant > 0.5, ex, ex - 1) + 127
    byte = np.clip(np.where(amax > 0, byte, 1), 1, 254)
    scaled = (w * np.exp2(127.0 - byte)[:, None, :]).reshape(k, n).astype(np.float32)
    by_word = np.ascontiguousarray(scaled.reshape(k // 512, 128, 4, n).transpose(0, 1, 3, 2))
    if fmt == "e4m3":
        words = by_word.astype(ml_dtypes.float8_e4m3fn).view(np.uint8)
    else:
        c = by_word.astype(ml_dtypes.float4_e2m1fn).view(np.uint8) & 0xF
        words = (c[..., 0::2] | (c[..., 1::2] << 4)).reshape(k // 512, 128, 2 * n)
    return np.ascontiguousarray(words), np.ascontiguousarray(byte.astype(np.uint8).reshape(k // 512, 16, n))


def unpack_weight(words, scales, fmt):
    g, _, n = scales.shape
    words = np.ascontiguousarray(words).reshape(g, 128, n, -1)
    if fmt == "e4m3":
        vals = words.view(ml_dtypes.float8_e4m3fn).astype(np.float64)
    else:
        nib = np.empty((g, 128, n, 4), np.uint8)
        nib[..., 0::2] = words & 0xF
        nib[..., 1::2] = words >> 4
        vals = E2M1[nib]
    vals = vals * np.repeat(np.exp2(scales.astype(np.float64) - 127.0), 8, axis=1)[..., None]
    return vals.transpose(0, 1, 3, 2).reshape(g * 512, n)


D, E, T, I, Q = 512, 512, 2048, 512, 128


def setup_inputs():
    n = np.random.standard_normal
    idx = np.random.permutation(T)[:I]
    fd = mx_kscale(D)
    fe = mx_kscale(E)
    keysp = pack_weight(n((D, T)) / fd[:, None], "e4m3")
    valsp = pack_weight(n((E, T)) / fe[:, None], "e4m3")
    return {
        "query": (n((D, Q)) * 0.8 / np.sqrt(D) * fd[:, None]).astype(np.float32),
        "keys_words": keysp[0],
        "keys_scales": keysp[1],
        "lean": (np.random.uniform(0.2, 0.6, (Q, 1))).astype(np.float32),
        "gout": (n((E, Q)) * 1 / np.sqrt(E) * fe[:, None]).astype(np.float32),
        "vals_words": valsp[0],
        "vals_scales": valsp[1],
        "dquery": (n((D, Q)) * 1.0 / np.sqrt(D) * fd[:, None]).astype(np.float32),
        "base": (0.5 * n((Q, T))).astype(np.float32),
        "offs": striped(idx),
    }


def reference(query, keys_words, keys_scales, lean, gout, vals_words, vals_scales, dquery, base, offs):
    idx = unstriped(offs)
    keysu = unpack_weight(keys_words, keys_scales, "e4m3")
    valsu = unpack_weight(vals_words, vals_scales, "e4m3")
    queryq = mxq(f64(query), 0, "e4m3")
    keysidxg = keysu[:, idx]
    a = queryq.T @ keysidxg
    dqueryq = mxq(f64(dquery), 0, "e4m3")
    ta = dqueryq.T @ keysidxg
    p = np.exp(a - np.max(a, axis=1, keepdims=True))
    r = p / np.sum(p, axis=1, keepdims=True)
    m0 = np.sum(r * a, axis=1, keepdims=True)
    goutq = mxq(f64(gout), 0, "e4m3")
    valsidxg = valsu[:, idx]
    c0 = goutq.T @ valsidxg
    dm0 = np.sum(c0 * r * f64(lean) * (-1.0), axis=1, keepdims=True)
    dr = c0 * ((a - m0) * f64(lean) + 1.0) + dm0 * a
    dp = dr / np.sum(p, axis=1, keepdims=True) + np.sum(dr * p / np.square(np.sum(p, axis=1, keepdims=True)) * (-1.0), axis=1, keepdims=True)
    tp = ta * p
    tr = (tp - np.sum(tp, axis=1, keepdims=True) * p / np.sum(p, axis=1, keepdims=True)) / np.sum(p, axis=1, keepdims=True)
    tm0 = np.sum(tr * a + ta * r, axis=1, keepdims=True)
    tdm0 = np.sum(tr * c0 * f64(lean) * (-1.0), axis=1, keepdims=True)
    tdr = (ta - tm0) * f64(lean) * c0 + tdm0 * a + ta * dm0
    tdp = (tdr - np.sum(tp, axis=1, keepdims=True) * dr / np.sum(p, axis=1, keepdims=True)) / np.sum(p, axis=1, keepdims=True) + np.sum((tdr * p + tp * dr - np.sum(tp, axis=1, keepdims=True) * np.sum(p, axis=1, keepdims=True) * 2.0 * dr * p / np.square(np.sum(p, axis=1, keepdims=True))) / np.square(np.sum(p, axis=1, keepdims=True)) * (-1.0), axis=1, keepdims=True)
    tda = tr * c0 * f64(lean) + tdm0 * r + tr * dm0 + tdp * p + tp * dp
    gs = tda * 512.0
    gf = np.zeros((Q, T))
    gf[:, idx] = gs
    y = f64(base) + gf
    return y

@@ -1,0 +1,174 @@
+from contextlib import ExitStack
+
+import concourse.mybir as mybir
+
+F32 = mybir.dt.float32
+BF16 = mybir.dt.bfloat16
+I32 = mybir.dt.int32
+U32 = mybir.dt.uint32
+U16 = mybir.dt.uint16
+U8 = mybir.dt.uint8
+FP8X4 = mybir.dt.float8_e4m3fn_x4
+ALU = mybir.AluOpType
+ACT = mybir.ActivationFunctionType
+AXIS = mybir.AxisListType
+
+P = 128
+PACK = 4
+TOKENS = 2048
+SLOTS = 512
+ROWS = 128
+GAIN = 512.0
+VALS_PLANE = 4
+OUT_CHUNK = 512
+
+FLOPS = 3 * 2 * 512 * ROWS * SLOTS
+
+
+def tile_attend_hvdirect_leaning_s_kernel(
+    tc, query, keys_words, keys_scales, lean, gout, vals_words, vals_scales, dquery, base, offs, out
+):
+    nc = tc.nc
+    with ExitStack() as ctx:
+        keep = ctx.enter_context(tc.tile_pool(name="keep", bufs=1))
+        psum = ctx.enter_context(tc.psum_pool(name="psum", bufs=1))
+
+        def wide(name):
+            return keep.tile([P, SLOTS], F32, name=name)
+
+        def column(name):
+            return keep.tile([P, 1], F32, name=name)
+
+        offsets = keep.tile([P, SLOTS // 16], U16, name="offsets")
+        nc.sync.dma_start(offsets[:], offs)
+
+        def load_scales(name, scales, first, queue):
+            pool_scales = keep.tile([P, TOKENS], U8, name=name)
+            nc.vector.memset(pool_scales[:].bitcast(I32), 0)
+            rows = scales[0].bitcast(I32)
+            for r in range(4):
+                queue.dma_start(pool_scales[first + r : P : 32, :].bitcast(I32), rows[r:16:4, :])
+            return pool_scales
+
+        def load_words(name, words, tag):
+            pool_words = keep.tile([P, TOKENS], I32, name=name, tag=tag)
+            nc.sync.dma_start(pool_words[:], words[0].rearrange("p n t -> p (n t)").bitcast(I32))
+            return pool_words
+
+        def load_rows(name, rows, tag):
+            raw = keep.tile([P, PACK, ROWS], F32, name=name, tag=tag)
+            nc.sync.dma_start(raw[:], rows.rearrange("(p j) w -> p j w", j=PACK))
+            return raw
+
+        def interleave(name, raw):
+            grouped = keep.tile([P, ROWS, PACK], BF16, name=name, align_bytes=64)
+            nc.scalar.activation(grouped[:], raw[:].rearrange("p j w -> p w j"), ACT.Copy)
+            return grouped
+
+        def quantize(name, grouped):
+            codes = keep.tile([P, ROWS], U32, name=name + "_codes", align_bytes=64)
+            scales = keep.tile([P, ROWS], U8, name=name + "_scales", align_bytes=64)
+            nc.vector.quantize_mx(
+                out=codes[:].bitcast(FP8X4), scales=scales[:], in_=grouped[:].rearrange("p w j -> p (w j)")
+            )
+            return codes, scales
+
+        def gather(name, window, dtype):
+            picked = keep.tile([P, SLOTS], dtype, name=name, align_bytes=64)
+            nc.vector.tensor_copy(picked[:], window.indirect(offsets[:]))
+            return picked
+
+        def product(name, rows, words, scales):
+            bank = psum.tile([P, SLOTS], F32, name=name)
+            nc.tensor.matmul_mx(
+                out=bank[:],
+                lhsT=rows[0][:].bitcast(FP8X4),
+                lhsT_scale=rows[1][:],
+                rhs=words[:].bitcast(FP8X4),
+                rhs_scale=scales,
+                start=True,
+                stop=True,
+            )
+            return bank
+
+        def fused(result, in0, scalar, in1, op0, op1, total=None):
+            nc.vector.scalar_tensor_tensor(
+                result[:], in0[:], scalar, in1[:], op0, op1, accum_out=None if total is None else total[:]
+            )
+
+        keys_pool_scales = load_scales("keys_pool_scales", keys_scales, 0, nc.scalar)
+        lean_col = column("lean_col")
+        nc.gpsimd.dma_start(lean_col[:], lean)
+        vals_pool_scales = load_scales("vals_pool_scales", vals_scales, VALS_PLANE, nc.gpsimd)
+        placed = keep.tile([P, TOKENS], F32, name="placed")
+        nc.vector.memset(placed[:], 0.0)
+
+        query_raw = load_rows("query_raw", query, "first")
+        keys_pool_words = load_words("keys_pool_words", keys_words, "keys")
+        dquery_raw = load_rows("dquery_raw", dquery, "second")
+
+        lean_up, lean_down, level = column("lean_up"), column("lean_down"), column("level")
+        nc.gpsimd.tensor_scalar(lean_up[:], lean_col[:], GAIN, 0.0, ALU.mult, ALU.add)
+        nc.gpsimd.tensor_scalar(lean_down[:], lean_col[:], -GAIN, 0.0, ALU.mult, ALU.add)
+        nc.gpsimd.tensor_scalar(level[:], lean_col[:], 2.0 * GAIN, GAIN, ALU.mult, ALU.add)
+
+        keys_s = gather("keys_s", keys_pool_scales[:], U8)
+        query_q = quantize("query", interleave("query_grouped", query_raw))
+        vals_pool_words = load_words("vals_pool_words", vals_words, "first")
+        keys_w = gather("keys_w", keys_pool_words[:].bitcast(U32), U32)
+        a = product("a", query_q, keys_w, keys_s[:])
+        dquery_q = quantize("dquery", interleave("dquery_grouped", dquery_raw))
+        gout_raw = load_rows("gout_raw", gout, "second")
+        ta = product("ta", dquery_q, keys_w, keys_s[:])
+
+        neg_max, p_sum, inv_sum = column("neg_max"), column("p_sum"), column("inv_sum")
+        nc.vector.tensor_reduce(neg_max[:], a[:], AXIS.X, ALU.max, negate=True)
+        p = wide("p")
+        nc.scalar.activation(p[:], a[:], ACT.Exp, bias=neg_max[:], accum_out=p_sum[:])
+        vals_s = gather("vals_s", vals_pool_scales[:], U8)
+        vals_w = gather("vals_w", vals_pool_words[:].bitcast(U32), U32)
+        base_sb = keep.tile([P, TOKENS], F32, name="base_sb", tag="first")
+        nc.sync.dma_start(base_sb[:], base)
+        nc.vector.reciprocal(inv_sum[:], p_sum[:])
+        r = wide("r")
+        nc.scalar.activation(r[:], p[:], ACT.Copy, scale=inv_sum[:])
+        gout_q = quantize("gout", interleave("gout_grouped", gout_raw))
+        c0 = product("c0", gout_q, vals_w, vals_s[VALS_PLANE:P, :])
+
+        spent = wide("spent")
+        ta_sum, ta_mean = column("ta_sum"), column("ta_mean")
+        fused(spent, ta, 1.0, p, ALU.mult, ALU.mult, ta_sum)
+        nc.scalar.activation(ta_mean[:], ta_sum[:], ACT.Copy, scale=inv_sum[:])
+        spent2 = wide("spent2")
+        a_sum, a_mean = column("a_sum"), column("a_mean")
+        fused(spent2, a, lean_up[:], p, ALU.mult, ALU.mult, a_sum)
+        nc.scalar.activation(a_mean[:], a_sum[:], ACT.Copy, scale=inv_sum[:])
+        tilt = wide("tilt")
+        nc.scalar.activation(tilt[:], a[:], ACT.Identity, bias=a_mean[:], scale=lean_down[:])
+
+        ru = wide("ru")
+        fused(ru, ta, ta_mean[:], r, ALU.subtract, ALU.mult)
+        rc, c_mean = wide("rc"), column("c_mean")
+        fused(rc, c0, 1.0, r, ALU.mult, ALU.mult, c_mean)
+        ruw, beta = wide("ruw"), column("beta")
+        fused(ruw, tilt, level[:], ru, ALU.subtract, ALU.mult, beta)
+        gamma = column("gamma")
+        fused(spent, c0, 1.0, ru, ALU.mult, ALU.mult, gamma)
+        tilt_gamma = wide("tilt_gamma")
+        nc.scalar.activation(tilt_gamma[:], tilt[:], ACT.Copy, scale=gamma[:])
+        lead = wide("lead")
+        fused(lead, r, beta[:], ruw, ALU.mult, ALU.subtract)
+        alpha = column("alpha")
+        fused(spent2, rc, 1.0, tilt, ALU.mult, ALU.mult, alpha)
+        main, kappa = wide("main"), column("kappa")
+        fused(main, c0, c_mean[:], lead, ALU.subtract, ALU.mult, kappa)
+        left, right = wide("left"), wide("right")
+        fused(left, ru, alpha[:], main, ALU.mult, ALU.add)
+        fused(right, tilt_gamma, kappa[:], r, ALU.subtract, ALU.mult)
+        nc.vector.tensor_tensor(placed[:].indirect(offsets[:]), left[:], right[:], ALU.add)
+
+        for k in range(TOKENS // OUT_CHUNK):
+            cols = slice(k * OUT_CHUNK, (k + 1) * OUT_CHUNK)
+            result = keep.tile([P, OUT_CHUNK], F32, name="result%d" % k)
+            nc.vector.tensor_tensor(result[:], placed[:, cols], base_sb[:, cols], ALU.add)
+            nc.sync.dma_start(out[:, cols], result[:])

@@ -42,27 +42,30 @@ def tile_attend_hvdirect_leaning_s_kernel(
         offsets = keep.tile([P, SLOTS // 16], U16, name="offsets")
         nc.sync.dma_start(offsets[:], offs)
 
-        def load_scales(name, scales, first, queue):
-            pool_scales = keep.tile([P, TOKENS], U8, name=name)
+        def zeroed_scales(name, tag):
+            pool_scales = keep.tile([P, TOKENS], U8, name=name, tag=tag, align_bytes=64)
             nc.vector.memset(pool_scales[:].bitcast(I32), 0)
-            rows = scales[0].bitcast(I32)
-            for r in range(4):
-                queue.dma_start(pool_scales[first + r : P : 32, :].bitcast(I32), rows[r:16:4, :])
             return pool_scales
 
-        def load_words(name, words, tag):
-            pool_words = keep.tile([P, TOKENS], I32, name=name, tag=tag)
+        def load_scales(pool_scales, scales, first, queues):
+            rows = scales[0].bitcast(I32)
+            for r in range(4):
+                queues[r % len(queues)].dma_start(pool_scales[first + r : P : 32, :].bitcast(I32), rows[r:16:4, :])
+
+        def load_words(pool_words, words):
             nc.sync.dma_start(pool_words[:], words[0].rearrange("p n t -> p (n t)").bitcast(I32))
             return pool_words
 
-        def load_rows(name, rows, tag):
-            raw = keep.tile([P, PACK, ROWS], F32, name=name, tag=tag)
+        def load_rows(raw, rows):
             nc.sync.dma_start(raw[:], rows.rearrange("(p j) w -> p j w", j=PACK))
             return raw
 
-        def interleave(name, raw):
+        def interleave(name, raw, on_vector=False):
             grouped = keep.tile([P, ROWS, PACK], BF16, name=name, align_bytes=64)
-            nc.scalar.activation(grouped[:], raw[:].rearrange("p j w -> p w j"), ACT.Copy)
+            if on_vector:
+                nc.vector.tensor_copy(grouped[:], raw[:].rearrange("p j w -> p w j"))
+            else:
+                nc.scalar.activation(grouped[:], raw[:].rearrange("p j w -> p w j"), ACT.Copy)
             return grouped
 
         def quantize(name, grouped):
@@ -73,8 +76,8 @@ def tile_attend_hvdirect_leaning_s_kernel(
             )
             return codes, scales
 
-        def gather(name, window, dtype):
-            picked = keep.tile([P, SLOTS], dtype, name=name, align_bytes=64)
+        def gather(name, window, dtype, tag):
+            picked = keep.tile([P, SLOTS], dtype, name=name, tag=tag, align_bytes=64)
             nc.vector.tensor_copy(picked[:], window.indirect(offsets[:]))
             return picked
 
@@ -96,44 +99,47 @@ def tile_attend_hvdirect_leaning_s_kernel(
                 result[:], in0[:], scalar, in1[:], op0, op1, accum_out=None if total is None else total[:]
             )
 
-        keys_pool_scales = load_scales("keys_pool_scales", keys_scales, 0, nc.scalar)
-        lean_col = column("lean_col")
-        nc.gpsimd.dma_start(lean_col[:], lean)
-        vals_pool_scales = load_scales("vals_pool_scales", vals_scales, VALS_PLANE, nc.gpsimd)
+        keys_pool_scales = zeroed_scales("keys_pool_scales", "keys_small")
+        vals_pool_scales = zeroed_scales("vals_pool_scales", "vals_small")
         placed = keep.tile([P, TOKENS], F32, name="placed")
         nc.vector.memset(placed[:], 0.0)
 
-        query_raw = load_rows("query_raw", query, "first")
-        keys_pool_words = load_words("keys_pool_words", keys_words, "keys")
-        dquery_raw = load_rows("dquery_raw", dquery, "second")
+        lean_col = column("lean_col")
+        nc.sync.dma_start(lean_col[:], lean)
+        query_raw = load_rows(keep.tile([P, PACK, ROWS], F32, name="query_raw"), query)
+        load_scales(keys_pool_scales, keys_scales, 0, [nc.sync, nc.scalar])
+        keys_pool_words = load_words(
+            keep.tile([P, TOKENS], I32, name="keys_pool_words", tag="keys_big", align_bytes=64), keys_words
+        )
+        dquery_raw = load_rows(keep.tile([P, PACK, ROWS], F32, name="dquery_raw"), dquery)
+        load_scales(vals_pool_scales, vals_scales, VALS_PLANE, [nc.sync])
+        gout_raw = load_rows(keep.tile([P, PACK, ROWS], F32, name="gout_raw"), gout)
+        vals_pool_words = load_words(keep.tile([P, TOKENS], I32, name="vals_pool_words"), vals_words)
+        base_sb = keep.tile([P, TOKENS], F32, name="base_sb")
+        nc.sync.dma_start(base_sb[:], base)
 
         lean_up, lean_down, level = column("lean_up"), column("lean_down"), column("level")
         nc.gpsimd.tensor_scalar(lean_up[:], lean_col[:], GAIN, 0.0, ALU.mult, ALU.add)
         nc.gpsimd.tensor_scalar(lean_down[:], lean_col[:], -GAIN, 0.0, ALU.mult, ALU.add)
         nc.gpsimd.tensor_scalar(level[:], lean_col[:], 2.0 * GAIN, GAIN, ALU.mult, ALU.add)
 
-        keys_s = gather("keys_s", keys_pool_scales[:], U8)
-        query_q = quantize("query", interleave("query_grouped", query_raw))
-        vals_pool_words = load_words("vals_pool_words", vals_words, "first")
-        keys_w = gather("keys_w", keys_pool_words[:].bitcast(U32), U32)
+        keys_s = gather("keys_s", keys_pool_scales[:], U8, "keys_s")
+        query_q = quantize("query", interleave("query_grouped", query_raw, True))
+        keys_w = gather("keys_w", keys_pool_words[:].bitcast(U32), U32, "keys_small")
         a = product("a", query_q, keys_w, keys_s[:])
         dquery_q = quantize("dquery", interleave("dquery_grouped", dquery_raw))
-        gout_raw = load_rows("gout_raw", gout, "second")
         ta = product("ta", dquery_q, keys_w, keys_s[:])
+        vals_s = gather("vals_s", vals_pool_scales[:], U8, "keys_big")
 
         neg_max, p_sum, inv_sum = column("neg_max"), column("p_sum"), column("inv_sum")
         nc.vector.tensor_reduce(neg_max[:], a[:], AXIS.X, ALU.max, negate=True)
+        gout_grouped = interleave("gout_grouped", gout_raw)
         p = wide("p")
         nc.scalar.activation(p[:], a[:], ACT.Exp, bias=neg_max[:], accum_out=p_sum[:])
-        vals_s = gather("vals_s", vals_pool_scales[:], U8)
-        vals_w = gather("vals_w", vals_pool_words[:].bitcast(U32), U32)
-        base_sb = keep.tile([P, TOKENS], F32, name="base_sb", tag="first")
-        nc.sync.dma_start(base_sb[:], base)
+        gout_q = quantize("gout", gout_grouped)
         nc.vector.reciprocal(inv_sum[:], p_sum[:])
         r = wide("r")
         nc.scalar.activation(r[:], p[:], ACT.Copy, scale=inv_sum[:])
-        gout_q = quantize("gout", interleave("gout_grouped", gout_raw))
-        c0 = product("c0", gout_q, vals_w, vals_s[VALS_PLANE:P, :])
 
         spent = wide("spent")
         ta_sum, ta_mean = column("ta_sum"), column("ta_mean")
@@ -145,6 +151,9 @@ def tile_attend_hvdirect_leaning_s_kernel(
         nc.scalar.activation(a_mean[:], a_sum[:], ACT.Copy, scale=inv_sum[:])
         tilt = wide("tilt")
         nc.scalar.activation(tilt[:], a[:], ACT.Identity, bias=a_mean[:], scale=lean_down[:])
+
+        vals_w = gather("vals_w", vals_pool_words[:].bitcast(U32), U32, "vals_w")
+        c0 = product("c0", gout_q, vals_w, vals_s[VALS_PLANE:P, :])
 
         ru = wide("ru")
         fused(ru, ta, ta_mean[:], r, ALU.subtract, ALU.mult)

from contextlib import ExitStack

import concourse.mybir as mybir

F32 = mybir.dt.float32
BF16 = mybir.dt.bfloat16
I32 = mybir.dt.int32
U32 = mybir.dt.uint32
U16 = mybir.dt.uint16
U8 = mybir.dt.uint8
FP8X4 = mybir.dt.float8_e4m3fn_x4
ALU = mybir.AluOpType
ACT = mybir.ActivationFunctionType
AXIS = mybir.AxisListType

P = 128
PACK = 4
TOKENS = 2048
SLOTS = 512
ROWS = 128
GAIN = 512.0
VALS_PLANE = 4
OUT_CHUNK = 512

FLOPS = 3 * 2 * 512 * ROWS * SLOTS


def tile_attend_hvdirect_leaning_s_kernel(
    tc, query, keys_words, keys_scales, lean, gout, vals_words, vals_scales, dquery, base, offs, out
):
    nc = tc.nc
    with ExitStack() as ctx:
        keep = ctx.enter_context(tc.tile_pool(name="keep", bufs=1))
        psum = ctx.enter_context(tc.psum_pool(name="psum", bufs=1))

        def wide(name):
            return keep.tile([P, SLOTS], F32, name=name)

        def column(name):
            return keep.tile([P, 1], F32, name=name)

        offsets = keep.tile([P, SLOTS // 16], U16, name="offsets")
        nc.sync.dma_start(offsets[:], offs)

        def zeroed_scales(name, tag):
            pool_scales = keep.tile([P, TOKENS], U8, name=name, tag=tag, align_bytes=64)
            nc.vector.memset(pool_scales[:].bitcast(I32), 0)
            return pool_scales

        def load_scales(pool_scales, scales, first, queues):
            rows = scales[0].bitcast(I32)
            for r in range(4):
                queues[r % len(queues)].dma_start(pool_scales[first + r : P : 32, :].bitcast(I32), rows[r:16:4, :])

        def load_words(pool_words, words):
            nc.sync.dma_start(pool_words[:], words[0].rearrange("p n t -> p (n t)").bitcast(I32))
            return pool_words

        def load_rows(raw, rows):
            nc.sync.dma_start(raw[:], rows.rearrange("(p j) w -> p j w", j=PACK))
            return raw

        def interleave(name, raw, on_vector=False):
            grouped = keep.tile([P, ROWS, PACK], BF16, name=name, align_bytes=64)
            if on_vector:
                nc.vector.tensor_copy(grouped[:], raw[:].rearrange("p j w -> p w j"))
            else:
                nc.scalar.activation(grouped[:], raw[:].rearrange("p j w -> p w j"), ACT.Copy)
            return grouped

        def quantize(name, grouped):
            codes = keep.tile([P, ROWS], U32, name=name + "_codes", align_bytes=64)
            scales = keep.tile([P, ROWS], U8, name=name + "_scales", align_bytes=64)
            nc.vector.quantize_mx(
                out=codes[:].bitcast(FP8X4), scales=scales[:], in_=grouped[:].rearrange("p w j -> p (w j)")
            )
            return codes, scales

        def gather(name, window, dtype, tag):
            picked = keep.tile([P, SLOTS], dtype, name=name, tag=tag, align_bytes=64)
            nc.vector.tensor_copy(picked[:], window.indirect(offsets[:]))
            return picked

        def product(name, rows, words, scales):
            bank = psum.tile([P, SLOTS], F32, name=name)
            nc.tensor.matmul_mx(
                out=bank[:],
                lhsT=rows[0][:].bitcast(FP8X4),
                lhsT_scale=rows[1][:],
                rhs=words[:].bitcast(FP8X4),
                rhs_scale=scales,
                start=True,
                stop=True,
            )
            return bank

        def fused(result, in0, scalar, in1, op0, op1, total=None):
            nc.vector.scalar_tensor_tensor(
                result[:], in0[:], scalar, in1[:], op0, op1, accum_out=None if total is None else total[:]
            )

        keys_pool_scales = zeroed_scales("keys_pool_scales", "keys_small")
        vals_pool_scales = zeroed_scales("vals_pool_scales", "vals_small")
        placed = keep.tile([P, TOKENS], F32, name="placed")
        nc.vector.memset(placed[:], 0.0)

        lean_col = column("lean_col")
        nc.sync.dma_start(lean_col[:], lean)
        query_raw = load_rows(keep.tile([P, PACK, ROWS], F32, name="query_raw"), query)
        load_scales(keys_pool_scales, keys_scales, 0, [nc.sync, nc.scalar])
        keys_pool_words = load_words(
            keep.tile([P, TOKENS], I32, name="keys_pool_words", tag="keys_big", align_bytes=64), keys_words
        )
        dquery_raw = load_rows(keep.tile([P, PACK, ROWS], F32, name="dquery_raw"), dquery)
        load_scales(vals_pool_scales, vals_scales, VALS_PLANE, [nc.sync])
        gout_raw = load_rows(keep.tile([P, PACK, ROWS], F32, name="gout_raw"), gout)
        vals_pool_words = load_words(keep.tile([P, TOKENS], I32, name="vals_pool_words"), vals_words)
        base_sb = keep.tile([P, TOKENS], F32, name="base_sb")
        nc.sync.dma_start(base_sb[:], base)

        lean_up, lean_down, level = column("lean_up"), column("lean_down"), column("level")
        nc.gpsimd.tensor_scalar(lean_up[:], lean_col[:], GAIN, 0.0, ALU.mult, ALU.add)
        nc.gpsimd.tensor_scalar(lean_down[:], lean_col[:], -GAIN, 0.0, ALU.mult, ALU.add)
        nc.gpsimd.tensor_scalar(level[:], lean_col[:], 2.0 * GAIN, GAIN, ALU.mult, ALU.add)

        keys_s = gather("keys_s", keys_pool_scales[:], U8, "keys_s")
        query_q = quantize("query", interleave("query_grouped", query_raw, True))
        keys_w = gather("keys_w", keys_pool_words[:].bitcast(U32), U32, "keys_small")
        a = product("a", query_q, keys_w, keys_s[:])
        dquery_q = quantize("dquery", interleave("dquery_grouped", dquery_raw))
        ta = product("ta", dquery_q, keys_w, keys_s[:])
        vals_s = gather("vals_s", vals_pool_scales[:], U8, "keys_big")

        neg_max, p_sum, inv_sum = column("neg_max"), column("p_sum"), column("inv_sum")
        nc.vector.tensor_reduce(neg_max[:], a[:], AXIS.X, ALU.max, negate=True)
        gout_grouped = interleave("gout_grouped", gout_raw)
        p = wide("p")
        nc.scalar.activation(p[:], a[:], ACT.Exp, bias=neg_max[:], accum_out=p_sum[:])
        gout_q = quantize("gout", gout_grouped)
        nc.vector.reciprocal(inv_sum[:], p_sum[:])
        r = wide("r")
        nc.scalar.activation(r[:], p[:], ACT.Copy, scale=inv_sum[:])

        spent = wide("spent")
        ta_sum, ta_mean = column("ta_sum"), column("ta_mean")
        fused(spent, ta, 1.0, p, ALU.mult, ALU.mult, ta_sum)
        nc.scalar.activation(ta_mean[:], ta_sum[:], ACT.Copy, scale=inv_sum[:])
        spent2 = wide("spent2")
        a_sum, a_mean = column("a_sum"), column("a_mean")
        fused(spent2, a, lean_up[:], p, ALU.mult, ALU.mult, a_sum)
        nc.scalar.activation(a_mean[:], a_sum[:], ACT.Copy, scale=inv_sum[:])
        tilt = wide("tilt")
        nc.scalar.activation(tilt[:], a[:], ACT.Identity, bias=a_mean[:], scale=lean_down[:])

        vals_w = gather("vals_w", vals_pool_words[:].bitcast(U32), U32, "vals_w")
        c0 = product("c0", gout_q, vals_w, vals_s[VALS_PLANE:P, :])

        ru = wide("ru")
        fused(ru, ta, ta_mean[:], r, ALU.subtract, ALU.mult)
        rc, c_mean = wide("rc"), column("c_mean")
        fused(rc, c0, 1.0, r, ALU.mult, ALU.mult, c_mean)
        ruw, beta = wide("ruw"), column("beta")
        fused(ruw, tilt, level[:], ru, ALU.subtract, ALU.mult, beta)
        gamma = column("gamma")
        fused(spent, c0, 1.0, ru, ALU.mult, ALU.mult, gamma)
        tilt_gamma = wide("tilt_gamma")
        nc.scalar.activation(tilt_gamma[:], tilt[:], ACT.Copy, scale=gamma[:])
        lead = wide("lead")
        fused(lead, r, beta[:], ruw, ALU.mult, ALU.subtract)
        alpha = column("alpha")
        fused(spent2, rc, 1.0, tilt, ALU.mult, ALU.mult, alpha)
        main, kappa = wide("main"), column("kappa")
        fused(main, c0, c_mean[:], lead, ALU.subtract, ALU.mult, kappa)
        left, right = wide("left"), wide("right")
        fused(left, ru, alpha[:], main, ALU.mult, ALU.add)
        fused(right, tilt_gamma, kappa[:], r, ALU.subtract, ALU.mult)
        nc.vector.tensor_tensor(placed[:].indirect(offsets[:]), left[:], right[:], ALU.add)

        for k in range(TOKENS // OUT_CHUNK):
            cols = slice(k * OUT_CHUNK, (k + 1) * OUT_CHUNK)
            result = keep.tile([P, OUT_CHUNK], F32, name="result%d" % k)
            nc.vector.tensor_tensor(result[:], placed[:, cols], base_sb[:, cols], ALU.add)
            nc.sync.dma_start(out[:, cols], result[:])
